import numpy as np
import ml_dtypes


def mxq(x, axis, fmt="e4m3"):
    dtype, down = {"e4m3": (ml_dtypes.float8_e4m3fn, 7), "e5m2": (ml_dtypes.float8_e5m2, 14)}[fmt]
    v = np.moveaxis(np.asarray(x, np.float32).astype(ml_dtypes.bfloat16).astype(np.float64), axis, -1)
    blocks = v.reshape(v.shape[:-1] + (-1, 32))
    amax = np.abs(blocks).max(-1, keepdims=True)
    byte = np.maximum(np.where(amax > 0, np.frexp(amax)[1] - 1 + 127, 0) - down, 1)
    scale = np.exp2(byte - 127.0)
    codes = (blocks / scale).astype(np.float32).astype(dtype).astype(np.float64)
    return np.moveaxis((codes * scale).reshape(v.shape), -1, axis)


WIDE = False


def mx_kscale(k):
    if not WIDE:
        return np.ones(k)
    levels = np.array([10, -10, 5, -5, 0])
    if k % 512:
        return np.exp2(np.random.permutation(np.resize(levels, k // 32))).repeat(32)
    a = np.empty((k // 512, 16))
    for p in range(k // 512):
        a[p, :8] = np.random.permutation(np.resize(levels, 8))
        for g in range(8):
            far = levels[np.abs(levels - a[p, g]) >= 10]
            a[p, g + 8] = far[np.random.randint(len(far))]
    return np.exp2(a.ravel()).repeat(32)


def f64(x):
    return np.asarray(x).astype(np.float64)


def striped(idx):
    return np.tile(np.asarray(idx).reshape(-1, 16).T, (8, 1)).astype(np.uint16)


def unstriped(offs):
    return offs[:16].T.reshape(-1).astype(np.int64)


E2M1 = np.array([0.0, 0.5, 1.0, 1.5, 2.0, 3.0, 4.0, 6.0, -0.0, -0.5, -1.0, -1.5, -2.0, -3.0, -4.0, -6.0])


def pack_weight(w, fmt):
    k, n = w.shape
    w = f64(np.asarray(w, np.float32).astype(ml_dtypes.bfloat16)).reshape(k // 32, 32, n)
    amax = np.abs(w).max(1)
    if fmt == "e4m3":
        byte = np.frexp(amax)[1] - 1 + 127 - 7
    else:
        mant, ex = np.frexp(amax / 6.0)
        byte = np.where(mant > 0.5, ex, ex - 1) + 127
    byte = np.clip(np.where(amax > 0, byte, 1), 1, 254)
    scaled = (w * np.exp2(127.0 - byte)[:, None, :]).reshape(k, n).astype(np.float32)
    by_word = np.ascontiguousarray(scaled.reshape(k // 512, 128, 4, n).transpose(0, 1, 3, 2))
    if fmt == "e4m3":
        words = by_word.astype(ml_dtypes.float8_e4m3fn).view(np.uint8)
    else:
        c = by_word.astype(ml_dtypes.float4_e2m1fn).view(np.uint8) & 0xF
        words = (c[..., 0::2] | (c[..., 1::2] << 4)).reshape(k // 512, 128, 2 * n)
    return np.ascontiguousarray(words), np.ascontiguousarray(byte.astype(np.uint8).reshape(k // 512, 16, n))


def unpack_weight(words, scales, fmt):
    g, _, n = scales.shape
    words = np.ascontiguousarray(words).reshape(g, 128, n, -1)
    if fmt == "e4m3":
        vals = words.view(ml_dtypes.float8_e4m3fn).astype(np.float64)
    else:
        nib = np.empty((g, 128, n, 4), np.uint8)
        nib[..., 0::2] = words & 0xF
        nib[..., 1::2] = words >> 4
        vals = E2M1[nib]
    vals = vals * np.repeat(np.exp2(scales.astype(np.float64) - 127.0), 8, axis=1)[..., None]
    return vals.transpose(0, 1, 3, 2).reshape(g * 512, n)


def sigmoid(v):
    return 1.0 / (1.0 + np.exp(-v))


D, E, T, I, Q, G = 512, 512, 2048, 512, 128, 64


def setup_inputs():
    n = np.random.standard_normal
    idx = np.random.permutation(T)[:I]
    fd = mx_kscale(D)
    fe = mx_kscale(E)
    keysp = pack_weight(n((D, T)) / fd[:, None], "e2m1")
    valsp = pack_weight(n((E, T)) / fe[:, None], "e2m1")
    return {
        "query": (n((D, Q)) * 0.8 / np.sqrt(D) * fd[:, None]).astype(np.float32),
        "keys_words": keysp[0],
        "keys_scales": keysp[1],
        "th": (np.random.uniform(1.8, 2.8, (Q, 1))).astype(np.float32),
        "gout": (n((E, Q)) * 1 / np.sqrt(E) * fe[:, None]).astype(np.float32),
        "vals_words": valsp[0],
        "vals_scales": valsp[1],
        "base": (0.5 * n((Q, I))).astype(np.float32),
        "offs": striped(idx),
    }


def reference(query, keys_words, keys_scales, th, gout, vals_words, vals_scales, base, offs):
    idx = unstriped(offs)
    keysu = unpack_weight(keys_words, keys_scales, "e2m1")
    valsu = unpack_weight(vals_words, vals_scales, "e2m1")
    queryq = mxq(f64(query), 0, "e4m3")
    keysidxg = keysu[:, idx]
    a = queryq.T @ keysidxg
    p = np.exp(a)
    s = p.reshape(Q, G, I // G).sum(axis=2)
    sh = sigmoid(np.log(s) - f64(th)) / s
    sr = np.repeat(sh, I // G, axis=1)
    goutq = mxq(f64(gout), 0, "e4m3")
    valsidxg = valsu[:, idx]
    c0 = goutq.T @ valsidxg
    dsr = c0 * p
    dsh = dsr.reshape(Q, G, I // G).sum(axis=2)
    ds = dsh / s * sigmoid(np.log(s) - f64(th)) * (1.0 - sigmoid(np.log(s) - f64(th))) / s - dsh * sigmoid(np.log(s) - f64(th)) / np.square(s)
    r1 = np.repeat(ds, I // G, axis=1)
    dp = c0 * sr + r1
    da = dp * p
    hda = da * 8.0 * 2.0 * 8.0
    hdp = hda * p
    hds = hdp.reshape(Q, G, I // G).sum(axis=2)
    hdsh = hds / s * (1.0 - sigmoid(np.log(s) - f64(th))) * sigmoid(np.log(s) - f64(th)) / s + hds * (-1.0) / np.square(s) * sigmoid(np.log(s) - f64(th))
    r51 = np.repeat(hdsh, I // G, axis=1)
    hsr = hdp * c0
    hsh = hsr.reshape(Q, G, I // G).sum(axis=2)
    hs = hds / s * (1.0 - sigmoid(np.log(s) - f64(th))) * dsh / s * sigmoid(np.log(s) - f64(th)) * (1.0 - sigmoid(np.log(s) - f64(th))) / s + hds / s * dsh / s * sigmoid(np.log(s) - f64(th)) * (-1.0) * sigmoid(np.log(s) - f64(th)) * (1.0 - sigmoid(np.log(s) - f64(th))) / s + hds * (-1.0) / np.square(s) * dsh * sigmoid(np.log(s) - f64(th)) * (1.0 - sigmoid(np.log(s) - f64(th))) / s + hds * (-1.0) * dsh * sigmoid(np.log(s) - f64(th)) / np.square(np.square(s)) * (-1.0) * s * 2.0 + hsh / s * sigmoid(np.log(s) - f64(th)) * (1.0 - sigmoid(np.log(s) - f64(th))) / s - hds / s * (1.0 - sigmoid(np.log(s) - f64(th))) * sigmoid(np.log(s) - f64(th)) * dsh / np.square(s) - hds * dsh / s * sigmoid(np.log(s) - f64(th)) * (1.0 - sigmoid(np.log(s) - f64(th))) / np.square(s) - hsh * sigmoid(np.log(s) - f64(th)) / np.square(s)
    r52 = np.repeat(hs, I // G, axis=1)
    hp = hda * dp + r51 * c0 + r52
    ha = hp * p
    y = ha + f64(base)
    return y

@@ -1,0 +1,165 @@
+import math
+from contextlib import ExitStack
+
+import concourse.mybir as mybir
+
+F32 = mybir.dt.float32
+BF16 = mybir.dt.bfloat16
+I32 = mybir.dt.int32
+U32 = mybir.dt.uint32
+U16 = mybir.dt.uint16
+U8 = mybir.dt.uint8
+FP8X4 = mybir.dt.float8_e4m3fn_x4
+FP4X4 = mybir.dt.float4_e2m1fn_x4
+ALU = mybir.AluOpType
+ACT = mybir.ActivationFunctionType
+AXIS_X = mybir.AxisListType.X
+
+P = 128
+PACK = 4
+TOKENS = 2048
+SLOTS = 512
+GROUP = 8
+HALVES = 2
+HALF = SLOTS // HALVES
+HALF_GROUPS = HALF // GROUP
+LIST_COLS = SLOTS // 16
+PENALTY = 128.0
+
+FLOPS = 2 * 2 * 512 * P * SLOTS
+
+
+def tile_attend_gpgatedgroups_kernel(tc, query, keys_words, keys_scales, th, gout, vals_words, vals_scales, base, offs, out):
+    nc = tc.nc
+    with ExitStack() as ctx:
+        pool = ctx.enter_context(tc.tile_pool(name="sbuf", bufs=1))
+        psum = ctx.enter_context(tc.psum_pool(name="psum", bufs=1))
+
+        def new(name, shape, dtype):
+            return pool.tile(shape, dtype, name=name, align_bytes=64)
+
+        def grouped(ap):
+            return ap.rearrange("p (g j) -> p g j", j=GROUP)
+
+        def spread(ap):
+            return ap.unsqueeze(2).to_broadcast([P, HALF_GROUPS, GROUP])
+
+        offsets = pool.tile([P, LIST_COLS], U16, name="offsets")
+        nc.sync.dma_start(offsets[:], offs)
+
+        def load_words(name, words):
+            tile = new(name, [P, TOKENS], U16)
+            nc.sync.dma_start(tile[:].bitcast(I32), words[0].bitcast(I32))
+            return tile
+
+        def load_scales(name, scales, queues):
+            tile = new(name, [P, TOKENS], U8)
+            nc.vector.memset(tile[:].bitcast(I32), 0)
+            for quad, queue in enumerate(queues):
+                queue.dma_start(tile[32 * quad : 32 * quad + 4, :].bitcast(I32), scales[0, 4 * quad : 4 * quad + 4, :].bitcast(I32))
+            return tile
+
+        def load_rows(name, rows, tag):
+            tile = pool.tile([P, PACK, P], F32, name=name, tag=tag, align_bytes=64)
+            nc.sync.dma_start(tile[:], rows.rearrange("(p j) w -> p j w", j=PACK))
+            return tile
+
+        key_words = load_words("key_words", keys_words)
+        key_scales = load_scales("key_scales", keys_scales, [nc.scalar] * 4)
+        query_raw = load_rows("query_raw", query, "query_then_base")
+        val_words = load_words("val_words", vals_words)
+        gout_raw = load_rows("gout_raw", gout, "gout_raw")
+        th_col = new("th_col", [P, 1], F32)
+        nc.gpsimd.dma_start(th_col[:], th)
+        val_scales = load_scales("val_scales", vals_scales, [nc.sync, nc.sync, nc.gpsimd, nc.gpsimd])
+
+        def quantise(name, raw):
+            woven = new(name + "_woven", [P, P, PACK], BF16)
+            nc.scalar.activation(woven[:], raw[:].rearrange("p j w -> p w j"), ACT.Copy)
+            codes = new(name + "_codes", [P, P], U32)
+            scales = new(name + "_scales", [P, P], U8)
+            nc.vector.quantize_mx(out=codes[:].bitcast(FP8X4), scales=scales[:], in_=woven[:].rearrange("p w j -> p (w j)"))
+            return codes, scales
+
+        def product(name, raw, words, scales):
+            picked_words = new(name + "_picked_words", [P, SLOTS], U16)
+            nc.vector.tensor_copy(picked_words[:], words[:].indirect(offsets[:]))
+            codes, code_scales = quantise(name, raw)
+            banks = []
+            for h in range(HALVES):
+                picked = new("%s_picked_scales%d" % (name, h), [P, HALF], U8)
+                cols = slice(h * LIST_COLS // HALVES, (h + 1) * LIST_COLS // HALVES)
+                nc.vector.tensor_copy(picked[:], scales[:].indirect(offsets[:, cols]))
+                bank = psum.tile([P, HALF], F32, name="%s_bank%d" % (name, h))
+                nc.tensor.matmul_mx(
+                    out=bank[:],
+                    lhsT=codes[:].bitcast(FP8X4),
+                    lhsT_scale=code_scales[:],
+                    rhs=picked_words[:, h * HALF : (h + 1) * HALF].bitcast(FP4X4),
+                    rhs_scale=picked[:],
+                    start=True,
+                    stop=True,
+                )
+                banks.append(bank)
+            return banks
+
+        score = product("score", query_raw, key_words, key_scales)
+        base_sb = pool.tile([P, SLOTS], F32, name="base_sb", tag="query_then_base", align_bytes=64)
+        nc.sync.dma_start(base_sb[:], base)
+        sink = new("sink", [P, 1], F32)
+        nc.scalar.activation(sink[:], th_col[:], ACT.Exp)
+        both = range(HALVES)
+        expo = [new("expo%d" % h, [P, HALF], F32) for h in both]
+        for h in both:
+            nc.scalar.activation(expo[h][:], score[h][:], ACT.Exp)
+        c0 = product("c0", gout_raw, val_words, val_scales)
+
+        total = [new("total%d" % h, [P, HALF_GROUPS], F32) for h in both]
+        denom = [new("denom%d" % h, [P, HALF_GROUPS], F32) for h in both]
+        recip = [new("recip%d" % h, [P, HALF_GROUPS], F32) for h in both]
+        pair = [new("pair%d" % h, [P, 2, HALF], F32) for h in both]
+        weighted = [new("weighted%d" % h, [P, HALF], F32) for h in both]
+        mean = [new("mean%d" % h, [P, HALF_GROUPS], F32) for h in both]
+        centred = [new("centred%d" % h, [P, HALF], F32) for h in both]
+        terms = [new("terms%d" % h, [P, 2, HALF], F32) for h in both]
+        sums = [new("sums%d" % h, [P, 2 * HALF_GROUPS], F32) for h in both]
+        direct = [new("direct%d" % h, [P, HALF], F32) for h in both]
+        back = [new("back%d" % h, [P, 2, HALF], F32) for h in both]
+        partial = [new("partial%d" % h, [P, HALF], F32) for h in both]
+        result = [new("result%d" % h, [P, HALF], F32) for h in both]
+
+        for h in both:
+            nc.vector.tensor_reduce(total[h][:], grouped(expo[h][:]), AXIS_X, ALU.add)
+        for h in both:
+            nc.vector.tensor_scalar(denom[h][:], total[h][:], sink[:], None, ALU.add)
+        for h in both:
+            nc.vector.reciprocal(recip[h][:], denom[h][:])
+        for h in both:
+            nc.vector.tensor_tensor(grouped(pair[h][:, 1, :]), grouped(expo[h][:]), spread(recip[h][:]), ALU.mult)
+        for h in both:
+            nc.vector.tensor_tensor(weighted[h][:], c0[h][:], pair[h][:, 1, :], ALU.mult)
+        for h in both:
+            nc.vector.tensor_reduce(mean[h][:], grouped(weighted[h][:]), AXIS_X, ALU.add)
+        for h in both:
+            nc.vector.tensor_tensor(grouped(centred[h][:]), grouped(c0[h][:]), spread(mean[h][:]), ALU.subtract)
+        for h in both:
+            nc.vector.tensor_tensor(pair[h][:, 0, :], centred[h][:], pair[h][:, 1, :], ALU.mult)
+        for h in both:
+            nc.scalar.activation(terms[h][:, 1, :], pair[h][:, 0, :], ACT.Square, scale=math.sqrt(PENALTY))
+            nc.vector.scalar_tensor_tensor(terms[h][:, 0, :], pair[h][:, 0, :], PENALTY, pair[h][:, 1, :], ALU.mult, ALU.mult)
+        for h in both:
+            nc.vector.tensor_reduce(sums[h][:], terms[h][:].rearrange("p s (g j) -> p (s g) j", j=GROUP), AXIS_X, ALU.add)
+        for h in both:
+            nc.vector.tensor_tensor(direct[h][:], terms[h][:, 1, :], base_sb[:, h * HALF : (h + 1) * HALF], ALU.add)
+        for h in both:
+            nc.vector.tensor_tensor(
+                back[h][:].rearrange("p s (g j) -> p (s g) j", j=GROUP),
+                pair[h][:].rearrange("p s (g j) -> p (s g) j", j=GROUP),
+                sums[h][:].unsqueeze(2).to_broadcast([P, 2 * HALF_GROUPS, GROUP]),
+                ALU.mult,
+            )
+        for h in both:
+            nc.vector.tensor_tensor(partial[h][:], direct[h][:], back[h][:, 0, :], ALU.subtract)
+        for h in both:
+            nc.vector.tensor_tensor(result[h][:], partial[h][:], back[h][:, 1, :], ALU.subtract)
+            nc.sync.dma_start(out[:, h * HALF : (h + 1) * HALF], result[h][:])

@@ -25,6 +25,7 @@ HALF = SLOTS // HALVES
 HALF_GROUPS = HALF // GROUP
 LIST_COLS = SLOTS // 16
 PENALTY = 128.0
+ROW = 12
 
 FLOPS = 2 * 2 * 512 * P * SLOTS
 
@@ -65,13 +66,13 @@ def tile_attend_gpgatedgroups_kernel(tc, query, keys_words, keys_scales, th, gou
             return tile
 
         key_words = load_words("key_words", keys_words)
+        val_words = load_words("val_words", vals_words)
+        th_col = new("th_col", [P, 1], F32)
+        nc.scalar.dma_start(th_col[:], th)
         key_scales = load_scales("key_scales", keys_scales, [nc.scalar] * 4)
         query_raw = load_rows("query_raw", query, "query_then_base")
-        val_words = load_words("val_words", vals_words)
         gout_raw = load_rows("gout_raw", gout, "gout_raw")
-        th_col = new("th_col", [P, 1], F32)
-        nc.gpsimd.dma_start(th_col[:], th)
-        val_scales = load_scales("val_scales", vals_scales, [nc.sync, nc.sync, nc.gpsimd, nc.gpsimd])
+        val_scales = load_scales("val_scales", vals_scales, [nc.sync] * 4)
 
         def quantise(name, raw):
             woven = new(name + "_woven", [P, P, PACK], BF16)
@@ -81,9 +82,12 @@ def tile_attend_gpgatedgroups_kernel(tc, query, keys_words, keys_scales, th, gou
             nc.vector.quantize_mx(out=codes[:].bitcast(FP8X4), scales=scales[:], in_=woven[:].rearrange("p w j -> p (w j)"))
             return codes, scales
 
-        def product(name, raw, words, scales):
+        def pick_words(name, words):
             picked_words = new(name + "_picked_words", [P, SLOTS], U16)
             nc.vector.tensor_copy(picked_words[:], words[:].indirect(offsets[:]))
+            return picked_words
+
+        def product(name, raw, picked_words, scales):
             codes, code_scales = quantise(name, raw)
             banks = []
             for h in range(HALVES):
@@ -103,18 +107,19 @@ def tile_attend_gpgatedgroups_kernel(tc, query, keys_words, keys_scales, th, gou
                 banks.append(bank)
             return banks
 
-        score = product("score", query_raw, key_words, key_scales)
+        key_picked = pick_words("score", key_words)
+        val_picked = pick_words("c0", val_words)
+        score = product("score", query_raw, key_picked, key_scales)
         base_sb = pool.tile([P, SLOTS], F32, name="base_sb", tag="query_then_base", align_bytes=64)
         nc.sync.dma_start(base_sb[:], base)
-        sink = new("sink", [P, 1], F32)
-        nc.scalar.activation(sink[:], th_col[:], ACT.Exp)
         both = range(HALVES)
-        expo = [new("expo%d" % h, [P, HALF], F32) for h in both]
+        expo = [new("expo%d" % h, [P, HALF_GROUPS, ROW], F32) for h in both]
         for h in both:
-            nc.scalar.activation(expo[h][:], score[h][:], ACT.Exp)
-        c0 = product("c0", gout_raw, val_words, val_scales)
+            nc.scalar.activation(expo[h][:, :, GROUP], th_col[:].to_broadcast([P, HALF_GROUPS]), ACT.Exp)
+        for h in both:
+            nc.scalar.activation(expo[h][:, :, 0:GROUP], grouped(score[h][:]), ACT.Exp)
+        c0 = product("c0", gout_raw, val_picked, val_scales)
 
-        total = [new("total%d" % h, [P, HALF_GROUPS], F32) for h in both]
         denom = [new("denom%d" % h, [P, HALF_GROUPS], F32) for h in both]
         recip = [new("recip%d" % h, [P, HALF_GROUPS], F32) for h in both]
         pair = [new("pair%d" % h, [P, 2, HALF], F32) for h in both]
@@ -129,13 +134,11 @@ def tile_attend_gpgatedgroups_kernel(tc, query, keys_words, keys_scales, th, gou
         result = [new("result%d" % h, [P, HALF], F32) for h in both]
 
         for h in both:
-            nc.vector.tensor_reduce(total[h][:], grouped(expo[h][:]), AXIS_X, ALU.add)
-        for h in both:
-            nc.vector.tensor_scalar(denom[h][:], total[h][:], sink[:], None, ALU.add)
+            nc.vector.tensor_reduce(denom[h][:], expo[h][:, :, 0 : GROUP + 1], AXIS_X, ALU.add)
         for h in both:
             nc.vector.reciprocal(recip[h][:], denom[h][:])
         for h in both:
-            nc.vector.tensor_tensor(grouped(pair[h][:, 1, :]), grouped(expo[h][:]), spread(recip[h][:]), ALU.mult)
+            nc.vector.tensor_tensor(grouped(pair[h][:, 1, :]), expo[h][:, :, 0:GROUP], spread(recip[h][:]), ALU.mult)
         for h in both:
             nc.vector.tensor_tensor(weighted[h][:], c0[h][:], pair[h][:, 1, :], ALU.mult)
         for h in both:

@@ -20,9 +20,8 @@ PACK = 4
 TOKENS = 2048
 SLOTS = 512
 GROUP = 8
-HALVES = 2
-HALF = SLOTS // HALVES
-HALF_GROUPS = HALF // GROUP
+PART_GROUPS = (28, 36)
+PART_COLS = (slice(0, PART_GROUPS[0] * GROUP), slice(PART_GROUPS[0] * GROUP, SLOTS))
 LIST_COLS = SLOTS // 16
 PENALTY = 128.0
 ROW = 12
@@ -35,18 +34,19 @@ def tile_attend_gpgatedgroups_kernel(tc, query, keys_words, keys_scales, th, gou
     with ExitStack() as ctx:
         pool = ctx.enter_context(tc.tile_pool(name="sbuf", bufs=1))
         psum = ctx.enter_context(tc.psum_pool(name="psum", bufs=1))
+        both = range(2)
 
-        def new(name, shape, dtype):
-            return pool.tile(shape, dtype, name=name, align_bytes=64)
+        def new(name, shape, dtype, tag=None):
+            return pool.tile(shape, dtype, name=name, tag=tag or name, align_bytes=64)
+
+        def per_part(name, lead, width):
+            return [new("%s%d" % (name, h), [P] + lead + [PART_GROUPS[h] * width], F32) for h in both]
 
         def grouped(ap):
             return ap.rearrange("p (g j) -> p g j", j=GROUP)
 
         def spread(ap):
-            return ap.unsqueeze(2).to_broadcast([P, HALF_GROUPS, GROUP])
-
-        offsets = pool.tile([P, LIST_COLS], U16, name="offsets")
-        nc.sync.dma_start(offsets[:], offs)
+            return ap.unsqueeze(2).to_broadcast([P, ap.shape[1], GROUP])
 
         def load_words(name, words):
             tile = new(name, [P, TOKENS], U16)
@@ -60,109 +60,112 @@ def tile_attend_gpgatedgroups_kernel(tc, query, keys_words, keys_scales, th, gou
                 queue.dma_start(tile[32 * quad : 32 * quad + 4, :].bitcast(I32), scales[0, 4 * quad : 4 * quad + 4, :].bitcast(I32))
             return tile
 
-        def load_rows(name, rows, tag):
-            tile = pool.tile([P, PACK, P], F32, name=name, tag=tag, align_bytes=64)
-            nc.sync.dma_start(tile[:], rows.rearrange("(p j) w -> p j w", j=PACK))
+        def load_rows(name, rows, queue):
+            tile = new(name, [P, PACK, P], F32)
+            queue.dma_start(tile[:], rows.rearrange("(p j) w -> p j w", j=PACK))
             return tile
 
-        key_words = load_words("key_words", keys_words)
-        val_words = load_words("val_words", vals_words)
+        offsets = pool.tile([P, LIST_COLS], U16, name="offsets")
+        nc.sync.dma_start(offsets[:], offs)
         th_col = new("th_col", [P, 1], F32)
         nc.scalar.dma_start(th_col[:], th)
+        key_words = load_words("key_words", keys_words)
+        val_words = load_words("val_words", vals_words)
         key_scales = load_scales("key_scales", keys_scales, [nc.scalar] * 4)
-        query_raw = load_rows("query_raw", query, "query_then_base")
-        gout_raw = load_rows("gout_raw", gout, "gout_raw")
+        query_raw = load_rows("query_raw", query, nc.sync)
+        gout_raw = load_rows("gout_raw", gout, nc.sync)
         val_scales = load_scales("val_scales", vals_scales, [nc.sync] * 4)
 
-        def quantise(name, raw):
+        def pick(name, window, dtype):
+            picked = new(name, [P, SLOTS], dtype)
+            nc.vector.tensor_copy(picked[:], window[:].indirect(offsets[:]))
+            return picked
+
+        key_picked = pick("key_picked", key_words, U16)
+        val_picked = pick("val_picked", val_words, U16)
+
+        def product(name, raw, words, scales):
+            picked_scales = pick(name + "_picked_scales", scales, U8)
             woven = new(name + "_woven", [P, P, PACK], BF16)
             nc.scalar.activation(woven[:], raw[:].rearrange("p j w -> p w j"), ACT.Copy)
             codes = new(name + "_codes", [P, P], U32)
-            scales = new(name + "_scales", [P, P], U8)
-            nc.vector.quantize_mx(out=codes[:].bitcast(FP8X4), scales=scales[:], in_=woven[:].rearrange("p w j -> p (w j)"))
-            return codes, scales
+            code_scales = new(name + "_scales", [P, P], U8)
+            nc.vector.quantize_mx(out=codes[:].bitcast(FP8X4), scales=code_scales[:], in_=woven[:].rearrange("p w j -> p (w j)"))
+            bank = psum.tile([P, SLOTS], F32, name=name + "_bank")
+            nc.tensor.matmul_mx(
+                out=bank[:],
+                lhsT=codes[:].bitcast(FP8X4),
+                lhsT_scale=code_scales[:],
+                rhs=words[:].bitcast(FP4X4),
+                rhs_scale=picked_scales[:],
+                start=True,
+                stop=True,
+            )
+            return [bank[:, cols] for cols in PART_COLS]
 
-        def pick_words(name, words):
-            picked_words = new(name + "_picked_words", [P, SLOTS], U16)
-            nc.vector.tensor_copy(picked_words[:], words[:].indirect(offsets[:]))
-            return picked_words
-
-        def product(name, raw, picked_words, scales):
-            codes, code_scales = quantise(name, raw)
-            banks = []
-            for h in range(HALVES):
-                picked = new("%s_picked_scales%d" % (name, h), [P, HALF], U8)
-                cols = slice(h * LIST_COLS // HALVES, (h + 1) * LIST_COLS // HALVES)
-                nc.vector.tensor_copy(picked[:], scales[:].indirect(offsets[:, cols]))
-                bank = psum.tile([P, HALF], F32, name="%s_bank%d" % (name, h))
-                nc.tensor.matmul_mx(
-                    out=bank[:],
-                    lhsT=codes[:].bitcast(FP8X4),
-                    lhsT_scale=code_scales[:],
-                    rhs=picked_words[:, h * HALF : (h + 1) * HALF].bitcast(FP4X4),
-                    rhs_scale=picked[:],
-                    start=True,
-                    stop=True,
-                )
-                banks.append(bank)
-            return banks
-
-        key_picked = pick_words("score", key_words)
-        val_picked = pick_words("c0", val_words)
+        expo = [new("expo%d" % h, [P, PART_GROUPS[h], ROW], F32) for h in both]
+        for h in both:
+            nc.scalar.activation(expo[h][:, :, GROUP], th_col[:].to_broadcast([P, PART_GROUPS[h]]), ACT.Exp)
         score = product("score", query_raw, key_picked, key_scales)
-        base_sb = pool.tile([P, SLOTS], F32, name="base_sb", tag="query_then_base", align_bytes=64)
+        base_sb = new("base_sb", [P, SLOTS], F32, tag="query_raw")
         nc.sync.dma_start(base_sb[:], base)
-        both = range(HALVES)
-        expo = [new("expo%d" % h, [P, HALF_GROUPS, ROW], F32) for h in both]
         for h in both:
-            nc.scalar.activation(expo[h][:, :, GROUP], th_col[:].to_broadcast([P, HALF_GROUPS]), ACT.Exp)
-        for h in both:
-            nc.scalar.activation(expo[h][:, :, 0:GROUP], grouped(score[h][:]), ACT.Exp)
+            nc.scalar.activation(expo[h][:, :, 0:GROUP], grouped(score[h]), ACT.Exp)
         c0 = product("c0", gout_raw, val_picked, val_scales)
 
-        denom = [new("denom%d" % h, [P, HALF_GROUPS], F32) for h in both]
-        recip = [new("recip%d" % h, [P, HALF_GROUPS], F32) for h in both]
-        pair = [new("pair%d" % h, [P, 2, HALF], F32) for h in both]
-        weighted = [new("weighted%d" % h, [P, HALF], F32) for h in both]
-        mean = [new("mean%d" % h, [P, HALF_GROUPS], F32) for h in both]
-        centred = [new("centred%d" % h, [P, HALF], F32) for h in both]
-        terms = [new("terms%d" % h, [P, 2, HALF], F32) for h in both]
-        sums = [new("sums%d" % h, [P, 2 * HALF_GROUPS], F32) for h in both]
-        direct = [new("direct%d" % h, [P, HALF], F32) for h in both]
-        back = [new("back%d" % h, [P, 2, HALF], F32) for h in both]
-        partial = [new("partial%d" % h, [P, HALF], F32) for h in both]
-        result = [new("result%d" % h, [P, HALF], F32) for h in both]
+        denom_all = new("denom", [P, SLOTS // GROUP], F32, tag="val_scales")
+        denom = [denom_all[:, 0 : PART_GROUPS[0]], denom_all[:, PART_GROUPS[0] :]]
+        recip = per_part("recip", [], 1)
+        share = per_part("share", [], GROUP)
+        weighted = per_part("weighted", [], GROUP)
+        mean = per_part("mean", [], 1)
+        centred = per_part("centred", [], GROUP)
+        grad = per_part("grad", [], GROUP)
+        terms = per_part("terms", [2], GROUP)
+        sums = per_part("sums", [2], 1)
+        direct = per_part("direct", [], GROUP)
+        result = per_part("result", [], GROUP)
 
         for h in both:
-            nc.vector.tensor_reduce(denom[h][:], expo[h][:, :, 0 : GROUP + 1], AXIS_X, ALU.add)
+            nc.vector.tensor_reduce(denom[h], expo[h][:, :, 0 : GROUP + 1], AXIS_X, ALU.add)
         for h in both:
-            nc.vector.reciprocal(recip[h][:], denom[h][:])
+            nc.vector.reciprocal(recip[h][:], denom[h])
         for h in both:
-            nc.vector.tensor_tensor(grouped(pair[h][:, 1, :]), expo[h][:, :, 0:GROUP], spread(recip[h][:]), ALU.mult)
+            nc.vector.tensor_tensor(grouped(share[h][:]), expo[h][:, :, 0:GROUP], spread(recip[h][:]), ALU.mult)
         for h in both:
-            nc.vector.tensor_tensor(weighted[h][:], c0[h][:], pair[h][:, 1, :], ALU.mult)
+            nc.vector.tensor_tensor(weighted[h][:], c0[h], share[h][:], ALU.mult)
         for h in both:
             nc.vector.tensor_reduce(mean[h][:], grouped(weighted[h][:]), AXIS_X, ALU.add)
         for h in both:
-            nc.vector.tensor_tensor(grouped(centred[h][:]), grouped(c0[h][:]), spread(mean[h][:]), ALU.subtract)
+            nc.vector.tensor_tensor(grouped(centred[h][:]), grouped(c0[h]), spread(mean[h][:]), ALU.subtract)
         for h in both:
-            nc.vector.tensor_tensor(pair[h][:, 0, :], centred[h][:], pair[h][:, 1, :], ALU.mult)
+            nc.vector.tensor_tensor(grad[h][:], centred[h][:], share[h][:], ALU.mult)
         for h in both:
-            nc.scalar.activation(terms[h][:, 1, :], pair[h][:, 0, :], ACT.Square, scale=math.sqrt(PENALTY))
-            nc.vector.scalar_tensor_tensor(terms[h][:, 0, :], pair[h][:, 0, :], PENALTY, pair[h][:, 1, :], ALU.mult, ALU.mult)
+            nc.scalar.activation(terms[h][:, 1, :], grad[h][:], ACT.Square, scale=math.sqrt(PENALTY))
+            nc.vector.scalar_tensor_tensor(terms[h][:, 0, :], grad[h][:], PENALTY, share[h][:], ALU.mult, ALU.mult)
         for h in both:
-            nc.vector.tensor_reduce(sums[h][:], terms[h][:].rearrange("p s (g j) -> p (s g) j", j=GROUP), AXIS_X, ALU.add)
-        for h in both:
-            nc.vector.tensor_tensor(direct[h][:], terms[h][:, 1, :], base_sb[:, h * HALF : (h + 1) * HALF], ALU.add)
-        for h in both:
-            nc.vector.tensor_tensor(
-                back[h][:].rearrange("p s (g j) -> p (s g) j", j=GROUP),
-                pair[h][:].rearrange("p s (g j) -> p (s g) j", j=GROUP),
-                sums[h][:].unsqueeze(2).to_broadcast([P, 2 * HALF_GROUPS, GROUP]),
-                ALU.mult,
+            nc.vector.tensor_reduce(
+                sums[h][:].rearrange("p s g -> p (s g)"), terms[h][:].rearrange("p s (g j) -> p (s g) j", j=GROUP), AXIS_X, ALU.add
             )
-        for h in both:
-            nc.vector.tensor_tensor(partial[h][:], direct[h][:], back[h][:, 0, :], ALU.subtract)
-        for h in both:
-            nc.vector.tensor_tensor(result[h][:], partial[h][:], back[h][:, 1, :], ALU.subtract)
-            nc.sync.dma_start(out[:, h * HALF : (h + 1) * HALF], result[h][:])
+        nc.gpsimd.tensor_tensor(direct[0][:], terms[0][:, 1, :], base_sb[:, PART_COLS[0]], ALU.add)
+
+        factor = new("factor", [P, PART_GROUPS[0] * GROUP], F32)
+        for g in range(PART_GROUPS[0]):
+            cols = slice(g * GROUP, (g + 1) * GROUP)
+            nc.scalar.activation(
+                factor[:, cols], centred[0][:, cols], ACT.Identity, scale=sums[0][:, 0, g : g + 1], bias=sums[0][:, 1, g : g + 1]
+            )
+
+        via_grad = new("via_grad", [P, PART_GROUPS[1] * GROUP], F32)
+        via_share = new("via_share", [P, PART_GROUPS[1] * GROUP], F32)
+        partial = new("partial", [P, PART_GROUPS[1] * GROUP], F32)
+        nc.vector.tensor_tensor(direct[1][:], terms[1][:, 1, :], base_sb[:, PART_COLS[1]], ALU.add)
+        nc.vector.tensor_tensor(grouped(via_grad[:]), grouped(grad[1][:]), spread(sums[1][:, 0, :]), ALU.mult)
+        nc.vector.tensor_tensor(grouped(via_share[:]), grouped(share[1][:]), spread(sums[1][:, 1, :]), ALU.mult)
+        nc.vector.tensor_tensor(partial[:], direct[1][:], via_grad[:], ALU.subtract)
+        back = new("back", [P, PART_GROUPS[0] * GROUP], F32)
+        nc.vector.tensor_tensor(back[:], factor[:], share[0][:], ALU.mult)
+        nc.vector.tensor_tensor(result[1][:], partial[:], via_share[:], ALU.subtract)
+        nc.sync.dma_start(out[:, PART_COLS[1]], result[1][:])
+        nc.vector.tensor_tensor(result[0][:], direct[0][:], back[:], ALU.subtract)
+        nc.sync.dma_start(out[:, PART_COLS[0]], result[0][:])

@@ -67,13 +67,13 @@ def tile_attend_gpgatedgroups_kernel(tc, query, keys_words, keys_scales, th, gou
 
         offsets = pool.tile([P, LIST_COLS], U16, name="offsets")
         nc.sync.dma_start(offsets[:], offs)
-        th_col = new("th_col", [P, 1], F32)
-        nc.scalar.dma_start(th_col[:], th)
         key_words = load_words("key_words", keys_words)
         val_words = load_words("val_words", vals_words)
-        key_scales = load_scales("key_scales", keys_scales, [nc.scalar] * 4)
+        key_scales = load_scales("key_scales", keys_scales, [nc.sync] * 4)
         query_raw = load_rows("query_raw", query, nc.sync)
         gout_raw = load_rows("gout_raw", gout, nc.sync)
+        th_col = new("th_col", [P, 1], F32)
+        nc.sync.dma_start(th_col[:], th)
         val_scales = load_scales("val_scales", vals_scales, [nc.sync] * 4)
 
         def pick(name, window, dtype):

@@ -17,16 +17,19 @@ AXIS_X = mybir.AxisListType.X
 
 P = 128
 PACK = 4
+FEATURES = P * PACK
+QUADRANT = 32
+SCALE_ROWS = 4
 TOKENS = 2048
 SLOTS = 512
 GROUP = 8
-PART_GROUPS = (28, 36)
-PART_COLS = (slice(0, PART_GROUPS[0] * GROUP), slice(PART_GROUPS[0] * GROUP, SLOTS))
 LIST_COLS = SLOTS // 16
 PENALTY = 128.0
-ROW = 12
+PART_GROUPS = (28, 36)
+PART_COLS = (slice(0, PART_GROUPS[0] * GROUP), slice(PART_GROUPS[0] * GROUP, SLOTS))
+EXPO_ROW = 12
 
-FLOPS = 2 * 2 * 512 * P * SLOTS
+FLOPS = 2 * 2 * FEATURES * P * SLOTS
 
 
 def tile_attend_gpgatedgroups_kernel(tc, query, keys_words, keys_scales, th, gout, vals_words, vals_scales, base, offs, out):
@@ -34,13 +37,13 @@ def tile_attend_gpgatedgroups_kernel(tc, query, keys_words, keys_scales, th, gou
     with ExitStack() as ctx:
         pool = ctx.enter_context(tc.tile_pool(name="sbuf", bufs=1))
         psum = ctx.enter_context(tc.psum_pool(name="psum", bufs=1))
-        both = range(2)
+        parts = range(len(PART_GROUPS))
 
         def new(name, shape, dtype, tag=None):
             return pool.tile(shape, dtype, name=name, tag=tag or name, align_bytes=64)
 
-        def per_part(name, lead, width):
-            return [new("%s%d" % (name, h), [P] + lead + [PART_GROUPS[h] * width], F32) for h in both]
+        def per_part(name, lead, per_group):
+            return [new("%s%d" % (name, h), [P] + lead + [PART_GROUPS[h] * per_group], F32) for h in parts]
 
         def grouped(ap):
             return ap.rearrange("p (g j) -> p g j", j=GROUP)
@@ -53,28 +56,29 @@ def tile_attend_gpgatedgroups_kernel(tc, query, keys_words, keys_scales, th, gou
             nc.sync.dma_start(tile[:].bitcast(I32), words[0].bitcast(I32))
             return tile
 
-        def load_scales(name, scales, queues):
+        def load_scales(name, scales):
             tile = new(name, [P, TOKENS], U8)
             nc.vector.memset(tile[:].bitcast(I32), 0)
-            for quad, queue in enumerate(queues):
-                queue.dma_start(tile[32 * quad : 32 * quad + 4, :].bitcast(I32), scales[0, 4 * quad : 4 * quad + 4, :].bitcast(I32))
+            for r in range(SCALE_ROWS):
+                rows = scales[0, r : FEATURES // 32 : SCALE_ROWS, :]
+                nc.sync.dma_start(tile[r:P:QUADRANT, :].bitcast(I32), rows.bitcast(I32))
             return tile
 
-        def load_rows(name, rows, queue):
+        def load_rows(name, rows):
             tile = new(name, [P, PACK, P], F32)
-            queue.dma_start(tile[:], rows.rearrange("(p j) w -> p j w", j=PACK))
+            nc.sync.dma_start(tile[:], rows.rearrange("(p t) q -> p t q", t=PACK))
             return tile
 
         offsets = pool.tile([P, LIST_COLS], U16, name="offsets")
-        nc.sync.dma_start(offsets[:], offs)
         key_words = load_words("key_words", keys_words)
+        nc.sync.dma_start(offsets[:], offs)
         val_words = load_words("val_words", vals_words)
-        key_scales = load_scales("key_scales", keys_scales, [nc.sync] * 4)
-        query_raw = load_rows("query_raw", query, nc.sync)
-        gout_raw = load_rows("gout_raw", gout, nc.sync)
+        key_scales = load_scales("key_scales", keys_scales)
+        query_raw = load_rows("query_raw", query)
+        gout_raw = load_rows("gout_raw", gout)
         th_col = new("th_col", [P, 1], F32)
         nc.sync.dma_start(th_col[:], th)
-        val_scales = load_scales("val_scales", vals_scales, [nc.sync] * 4)
+        val_scales = load_scales("val_scales", vals_scales)
 
         def pick(name, window, dtype):
             picked = new(name, [P, SLOTS], dtype)
@@ -84,32 +88,32 @@ def tile_attend_gpgatedgroups_kernel(tc, query, keys_words, keys_scales, th, gou
         key_picked = pick("key_picked", key_words, U16)
         val_picked = pick("val_picked", val_words, U16)
 
-        def product(name, raw, words, scales):
-            picked_scales = pick(name + "_picked_scales", scales, U8)
+        def product(name, raw, picked_words, pool_scales):
+            picked_scales = pick(name + "_picked_scales", pool_scales, U8)
             woven = new(name + "_woven", [P, P, PACK], BF16)
-            nc.scalar.activation(woven[:], raw[:].rearrange("p j w -> p w j"), ACT.Copy)
+            nc.scalar.activation(woven[:], raw[:].rearrange("p t q -> p q t"), ACT.Copy)
             codes = new(name + "_codes", [P, P], U32)
             code_scales = new(name + "_scales", [P, P], U8)
-            nc.vector.quantize_mx(out=codes[:].bitcast(FP8X4), scales=code_scales[:], in_=woven[:].rearrange("p w j -> p (w j)"))
+            nc.vector.quantize_mx(out=codes[:].bitcast(FP8X4), scales=code_scales[:], in_=woven[:].rearrange("p q t -> p (q t)"))
             bank = psum.tile([P, SLOTS], F32, name=name + "_bank")
             nc.tensor.matmul_mx(
                 out=bank[:],
                 lhsT=codes[:].bitcast(FP8X4),
                 lhsT_scale=code_scales[:],
-                rhs=words[:].bitcast(FP4X4),
+                rhs=picked_words[:].bitcast(FP4X4),
                 rhs_scale=picked_scales[:],
                 start=True,
                 stop=True,
             )
             return [bank[:, cols] for cols in PART_COLS]
 
-        expo = [new("expo%d" % h, [P, PART_GROUPS[h], ROW], F32) for h in both]
-        for h in both:
+        expo = [new("expo%d" % h, [P, PART_GROUPS[h], EXPO_ROW], F32) for h in parts]
+        for h in parts:
             nc.scalar.activation(expo[h][:, :, GROUP], th_col[:].to_broadcast([P, PART_GROUPS[h]]), ACT.Exp)
         score = product("score", query_raw, key_picked, key_scales)
         base_sb = new("base_sb", [P, SLOTS], F32, tag="query_raw")
         nc.sync.dma_start(base_sb[:], base)
-        for h in both:
+        for h in parts:
             nc.scalar.activation(expo[h][:, :, 0:GROUP], grouped(score[h]), ACT.Exp)
         c0 = product("c0", gout_raw, val_picked, val_scales)
 
@@ -126,29 +130,29 @@ def tile_attend_gpgatedgroups_kernel(tc, query, keys_words, keys_scales, th, gou
         direct = per_part("direct", [], GROUP)
         result = per_part("result", [], GROUP)
 
-        for h in both:
+        for h in parts:
             nc.vector.tensor_reduce(denom[h], expo[h][:, :, 0 : GROUP + 1], AXIS_X, ALU.add)
-        for h in both:
+        for h in parts:
             nc.vector.reciprocal(recip[h][:], denom[h])
-        for h in both:
+        for h in parts:
             nc.vector.tensor_tensor(grouped(share[h][:]), expo[h][:, :, 0:GROUP], spread(recip[h][:]), ALU.mult)
-        for h in both:
+        for h in parts:
             nc.vector.tensor_tensor(weighted[h][:], c0[h], share[h][:], ALU.mult)
-        for h in both:
+        for h in parts:
             nc.vector.tensor_reduce(mean[h][:], grouped(weighted[h][:]), AXIS_X, ALU.add)
-        for h in both:
+        for h in parts:
             nc.vector.tensor_tensor(grouped(centred[h][:]), grouped(c0[h]), spread(mean[h][:]), ALU.subtract)
-        for h in both:
+        for h in parts:
             nc.vector.tensor_tensor(grad[h][:], centred[h][:], share[h][:], ALU.mult)
-        for h in both:
+        for h in parts:
             nc.scalar.activation(terms[h][:, 1, :], grad[h][:], ACT.Square, scale=math.sqrt(PENALTY))
             nc.vector.scalar_tensor_tensor(terms[h][:, 0, :], grad[h][:], PENALTY, share[h][:], ALU.mult, ALU.mult)
-        for h in both:
+        for h in parts:
             nc.vector.tensor_reduce(
                 sums[h][:].rearrange("p s g -> p (s g)"), terms[h][:].rearrange("p s (g j) -> p (s g) j", j=GROUP), AXIS_X, ALU.add
             )
-        nc.gpsimd.tensor_tensor(direct[0][:], terms[0][:, 1, :], base_sb[:, PART_COLS[0]], ALU.add)
 
+        nc.gpsimd.tensor_tensor(direct[0][:], terms[0][:, 1, :], base_sb[:, PART_COLS[0]], ALU.add)
         factor = new("factor", [P, PART_GROUPS[0] * GROUP], F32)
         for g in range(PART_GROUPS[0]):
             cols = slice(g * GROUP, (g + 1) * GROUP)
@@ -163,9 +167,9 @@ def tile_attend_gpgatedgroups_kernel(tc, query, keys_words, keys_scales, th, gou
         nc.vector.tensor_tensor(grouped(via_grad[:]), grouped(grad[1][:]), spread(sums[1][:, 0, :]), ALU.mult)
         nc.vector.tensor_tensor(grouped(via_share[:]), grouped(share[1][:]), spread(sums[1][:, 1, :]), ALU.mult)
         nc.vector.tensor_tensor(partial[:], direct[1][:], via_grad[:], ALU.subtract)
-        back = new("back", [P, PART_GROUPS[0] * GROUP], F32)
-        nc.vector.tensor_tensor(back[:], factor[:], share[0][:], ALU.mult)
+        via_factor = new("via_factor", [P, PART_GROUPS[0] * GROUP], F32)
+        nc.vector.tensor_tensor(via_factor[:], factor[:], share[0][:], ALU.mult)
         nc.vector.tensor_tensor(result[1][:], partial[:], via_share[:], ALU.subtract)
         nc.sync.dma_start(out[:, PART_COLS[1]], result[1][:])
-        nc.vector.tensor_tensor(result[0][:], direct[0][:], back[:], ALU.subtract)
+        nc.vector.tensor_tensor(result[0][:], direct[0][:], via_factor[:], ALU.subtract)
         nc.sync.dma_start(out[:, PART_COLS[0]], result[0][:])

import math
from contextlib import ExitStack

import concourse.mybir as mybir

F32 = mybir.dt.float32
BF16 = mybir.dt.bfloat16
I32 = mybir.dt.int32
U32 = mybir.dt.uint32
U16 = mybir.dt.uint16
U8 = mybir.dt.uint8
FP8X4 = mybir.dt.float8_e4m3fn_x4
FP4X4 = mybir.dt.float4_e2m1fn_x4
ALU = mybir.AluOpType
ACT = mybir.ActivationFunctionType
AXIS_X = mybir.AxisListType.X

P = 128
PACK = 4
FEATURES = P * PACK
QUADRANT = 32
SCALE_ROWS = 4
TOKENS = 2048
SLOTS = 512
GROUP = 8
LIST_COLS = SLOTS // 16
PENALTY = 128.0
PART_GROUPS = (28, 36)
PART_COLS = (slice(0, PART_GROUPS[0] * GROUP), slice(PART_GROUPS[0] * GROUP, SLOTS))
EXPO_ROW = 12

FLOPS = 2 * 2 * FEATURES * P * SLOTS


def tile_attend_gpgatedgroups_kernel(tc, query, keys_words, keys_scales, th, gout, vals_words, vals_scales, base, offs, out):
    nc = tc.nc
    with ExitStack() as ctx:
        pool = ctx.enter_context(tc.tile_pool(name="sbuf", bufs=1))
        psum = ctx.enter_context(tc.psum_pool(name="psum", bufs=1))
        parts = range(len(PART_GROUPS))

        def new(name, shape, dtype, tag=None):
            return pool.tile(shape, dtype, name=name, tag=tag or name, align_bytes=64)

        def per_part(name, lead, per_group):
            return [new("%s%d" % (name, h), [P] + lead + [PART_GROUPS[h] * per_group], F32) for h in parts]

        def grouped(ap):
            return ap.rearrange("p (g j) -> p g j", j=GROUP)

        def spread(ap):
            return ap.unsqueeze(2).to_broadcast([P, ap.shape[1], GROUP])

        def load_words(name, words):
            tile = new(name, [P, TOKENS], U16)
            nc.sync.dma_start(tile[:].bitcast(I32), words[0].bitcast(I32))
            return tile

        def load_scales(name, scales):
            tile = new(name, [P, TOKENS], U8)
            nc.vector.memset(tile[:].bitcast(I32), 0)
            for r in range(SCALE_ROWS):
                rows = scales[0, r : FEATURES // 32 : SCALE_ROWS, :]
                nc.sync.dma_start(tile[r:P:QUADRANT, :].bitcast(I32), rows.bitcast(I32))
            return tile

        def load_rows(name, rows):
            tile = new(name, [P, PACK, P], F32)
            nc.sync.dma_start(tile[:], rows.rearrange("(p t) q -> p t q", t=PACK))
            return tile

        offsets = pool.tile([P, LIST_COLS], U16, name="offsets")
        key_words = load_words("key_words", keys_words)
        nc.sync.dma_start(offsets[:], offs)
        val_words = load_words("val_words", vals_words)
        key_scales = load_scales("key_scales", keys_scales)
        query_raw = load_rows("query_raw", query)
        gout_raw = load_rows("gout_raw", gout)
        th_col = new("th_col", [P, 1], F32)
        nc.sync.dma_start(th_col[:], th)
        val_scales = load_scales("val_scales", vals_scales)

        def pick(name, window, dtype):
            picked = new(name, [P, SLOTS], dtype)
            nc.vector.tensor_copy(picked[:], window[:].indirect(offsets[:]))
            return picked

        key_picked = pick("key_picked", key_words, U16)
        val_picked = pick("val_picked", val_words, U16)

        def product(name, raw, picked_words, pool_scales):
            picked_scales = pick(name + "_picked_scales", pool_scales, U8)
            woven = new(name + "_woven", [P, P, PACK], BF16)
            nc.scalar.activation(woven[:], raw[:].rearrange("p t q -> p q t"), ACT.Copy)
            codes = new(name + "_codes", [P, P], U32)
            code_scales = new(name + "_scales", [P, P], U8)
            nc.vector.quantize_mx(out=codes[:].bitcast(FP8X4), scales=code_scales[:], in_=woven[:].rearrange("p q t -> p (q t)"))
            bank = psum.tile([P, SLOTS], F32, name=name + "_bank")
            nc.tensor.matmul_mx(
                out=bank[:],
                lhsT=codes[:].bitcast(FP8X4),
                lhsT_scale=code_scales[:],
                rhs=picked_words[:].bitcast(FP4X4),
                rhs_scale=picked_scales[:],
                start=True,
                stop=True,
            )
            return [bank[:, cols] for cols in PART_COLS]

        expo = [new("expo%d" % h, [P, PART_GROUPS[h], EXPO_ROW], F32) for h in parts]
        for h in parts:
            nc.scalar.activation(expo[h][:, :, GROUP], th_col[:].to_broadcast([P, PART_GROUPS[h]]), ACT.Exp)
        score = product("score", query_raw, key_picked, key_scales)
        base_sb = new("base_sb", [P, SLOTS], F32, tag="query_raw")
        nc.sync.dma_start(base_sb[:], base)
        for h in parts:
            nc.scalar.activation(expo[h][:, :, 0:GROUP], grouped(score[h]), ACT.Exp)
        c0 = product("c0", gout_raw, val_picked, val_scales)

        denom_all = new("denom", [P, SLOTS // GROUP], F32, tag="val_scales")
        denom = [denom_all[:, 0 : PART_GROUPS[0]], denom_all[:, PART_GROUPS[0] :]]
        recip = per_part("recip", [], 1)
        share = per_part("share", [], GROUP)
        weighted = per_part("weighted", [], GROUP)
        mean = per_part("mean", [], 1)
        centred = per_part("centred", [], GROUP)
        grad = per_part("grad", [], GROUP)
        terms = per_part("terms", [2], GROUP)
        sums = per_part("sums", [2], 1)
        direct = per_part("direct", [], GROUP)
        result = per_part("result", [], GROUP)

        for h in parts:
            nc.vector.tensor_reduce(denom[h], expo[h][:, :, 0 : GROUP + 1], AXIS_X, ALU.add)
        for h in parts:
            nc.vector.reciprocal(recip[h][:], denom[h])
        for h in parts:
            nc.vector.tensor_tensor(grouped(share[h][:]), expo[h][:, :, 0:GROUP], spread(recip[h][:]), ALU.mult)
        for h in parts:
            nc.vector.tensor_tensor(weighted[h][:], c0[h], share[h][:], ALU.mult)
        for h in parts:
            nc.vector.tensor_reduce(mean[h][:], grouped(weighted[h][:]), AXIS_X, ALU.add)
        for h in parts:
            nc.vector.tensor_tensor(grouped(centred[h][:]), grouped(c0[h]), spread(mean[h][:]), ALU.subtract)
        for h in parts:
            nc.vector.tensor_tensor(grad[h][:], centred[h][:], share[h][:], ALU.mult)
        for h in parts:
            nc.scalar.activation(terms[h][:, 1, :], grad[h][:], ACT.Square, scale=math.sqrt(PENALTY))
            nc.vector.scalar_tensor_tensor(terms[h][:, 0, :], grad[h][:], PENALTY, share[h][:], ALU.mult, ALU.mult)
        for h in parts:
            nc.vector.tensor_reduce(
                sums[h][:].rearrange("p s g -> p (s g)"), terms[h][:].rearrange("p s (g j) -> p (s g) j", j=GROUP), AXIS_X, ALU.add
            )

        nc.gpsimd.tensor_tensor(direct[0][:], terms[0][:, 1, :], base_sb[:, PART_COLS[0]], ALU.add)
        factor = new("factor", [P, PART_GROUPS[0] * GROUP], F32)
        for g in range(PART_GROUPS[0]):
            cols = slice(g * GROUP, (g + 1) * GROUP)
            nc.scalar.activation(
                factor[:, cols], centred[0][:, cols], ACT.Identity, scale=sums[0][:, 0, g : g + 1], bias=sums[0][:, 1, g : g + 1]
            )

        via_grad = new("via_grad", [P, PART_GROUPS[1] * GROUP], F32)
        via_share = new("via_share", [P, PART_GROUPS[1] * GROUP], F32)
        partial = new("partial", [P, PART_GROUPS[1] * GROUP], F32)
        nc.vector.tensor_tensor(direct[1][:], terms[1][:, 1, :], base_sb[:, PART_COLS[1]], ALU.add)
        nc.vector.tensor_tensor(grouped(via_grad[:]), grouped(grad[1][:]), spread(sums[1][:, 0, :]), ALU.mult)
        nc.vector.tensor_tensor(grouped(via_share[:]), grouped(share[1][:]), spread(sums[1][:, 1, :]), ALU.mult)
        nc.vector.tensor_tensor(partial[:], direct[1][:], via_grad[:], ALU.subtract)
        via_factor = new("via_factor", [P, PART_GROUPS[0] * GROUP], F32)
        nc.vector.tensor_tensor(via_factor[:], factor[:], share[0][:], ALU.mult)
        nc.vector.tensor_tensor(result[1][:], partial[:], via_share[:], ALU.subtract)
        nc.sync.dma_start(out[:, PART_COLS[1]], result[1][:])
        nc.vector.tensor_tensor(result[0][:], direct[0][:], via_factor[:], ALU.subtract)
        nc.sync.dma_start(out[:, PART_COLS[0]], result[0][:])
